import numpy as np
import ml_dtypes


def mxq(x, axis, fmt="e4m3"):
    dtype, down = {"e4m3": (ml_dtypes.float8_e4m3fn, 7), "e5m2": (ml_dtypes.float8_e5m2, 14)}[fmt]
    v = np.moveaxis(np.asarray(x, np.float32).astype(ml_dtypes.bfloat16).astype(np.float64), axis, -1)
    blocks = v.reshape(v.shape[:-1] + (-1, 32))
    amax = np.abs(blocks).max(-1, keepdims=True)
    byte = np.maximum(np.where(amax > 0, np.frexp(amax)[1] - 1 + 127, 0) - down, 1)
    scale = np.exp2(byte - 127.0)
    codes = (blocks / scale).astype(np.float32).astype(dtype).astype(np.float64)
    return np.moveaxis((codes * scale).reshape(v.shape), -1, axis)


WIDE = False


def mx_kscale(k):
    if not WIDE:
        return np.ones(k)
    levels = np.array([10, -10, 5, -5, 0])
    if k % 512:
        return np.exp2(np.random.permutation(np.resize(levels, k // 32))).repeat(32)
    a = np.empty((k // 512, 16))
    for p in range(k // 512):
        a[p, :8] = np.random.permutation(np.resize(levels, 8))
        for g in range(8):
            far = levels[np.abs(levels - a[p, g]) >= 10]
            a[p, g + 8] = far[np.random.randint(len(far))]
    return np.exp2(a.ravel()).repeat(32)


def f64(x):
    return np.asarray(x).astype(np.float64)


def striped(idx):
    return np.tile(idx.reshape(-1, 16).T, (8, 1)).astype(np.uint16)


def unstriped(offs):
    return offs[:16].T.reshape(-1).astype(np.int64)


E2M1 = np.array([0.0, 0.5, 1.0, 1.5, 2.0, 3.0, 4.0, 6.0, -0.0, -0.5, -1.0, -1.5, -2.0, -3.0, -4.0, -6.0])


def pack_weight(w, fmt):
    k, n = w.shape
    w = f64(np.asarray(w, np.float32).astype(ml_dtypes.bfloat16)).reshape(k // 32, 32, n)
    amax = np.abs(w).max(1)
    if fmt == "e4m3":
        byte = np.frexp(amax)[1] - 1 + 127 - 7
    else:
        mant, ex = np.frexp(amax / 6.0)
        byte = np.where(mant > 0.5, ex, ex - 1) + 127
    byte = np.clip(np.where(amax > 0, byte, 1), 1, 254)
    scaled = (w * np.exp2(127.0 - byte)[:, None, :]).reshape(k, n).astype(np.float32)
    by_word = np.ascontiguousarray(scaled.reshape(k // 512, 128, 4, n).transpose(0, 1, 3, 2))
    if fmt == "e4m3":
        words = by_word.astype(ml_dtypes.float8_e4m3fn).view(np.uint8)
    else:
        c = by_word.astype(ml_dtypes.float4_e2m1fn).view(np.uint8) & 0xF
        words = (c[..., 0::2] | (c[..., 1::2] << 4)).reshape(k // 512, 128, 2 * n)
    return np.ascontiguousarray(words), np.ascontiguousarray(byte.astype(np.uint8).reshape(k // 512, 16, n))


def unpack_weight(words, scales, fmt):
    g, _, n = scales.shape
    words = np.ascontiguousarray(words).reshape(g, 128, n, -1)
    if fmt == "e4m3":
        vals = words.view(ml_dtypes.float8_e4m3fn).astype(np.float64)
    else:
        nib = np.empty((g, 128, n, 4), np.uint8)
        nib[..., 0::2] = words & 0xF
        nib[..., 1::2] = words >> 4
        vals = E2M1[nib]
    vals = vals * np.repeat(np.exp2(scales.astype(np.float64) - 127.0), 8, axis=1)[..., None]
    return vals.transpose(0, 1, 3, 2).reshape(g * 512, n)


def gelu(v):
    return 0.5 * v * (1.0 + np.tanh(np.sqrt(2.0 / np.pi) * (v + 0.044715 * v**3)))


K, T, S, H, T2, P, N = 1536, 4096, 1024, 1024, 2048, 512, 384

def setup_inputs():
    n = np.random.standard_normal
    s = mx_kscale(K)[:, None]
    u = mx_kscale(H)[:, None]
    tab_words, tab_scales = pack_weight(n((K, T)) * s, "e4m3")
    w1 = (n((K, H)) / s / np.sqrt(K)).astype(np.float32)
    w4_words, w4_scales = pack_weight(n((H, N)) / u / np.sqrt(H), "e2m1")
    fit = np.random.uniform(0.5, 2.5, (H, S)).astype(np.float32)
    gain = (1.3 * np.exp(0.3 * n(H)) * u[:, 0]).astype(np.float32)
    wgs = np.exp(0.3 * n((128, S))).astype(np.float32)
    page0 = (n((H, T2)) * u).astype(np.float32)
    base = (0.7 * n(N)).astype(np.float32)
    perm = np.random.permutation(T2)
    return {"tab_words": tab_words, "tab_scales": tab_scales,
            "offs": striped(np.random.permutation(T)[:S]),
            "w1": w1, "fit": fit, "gain": gain, "wgs": wgs, "page0": page0,
            "offs2": striped(np.random.permutation(T2)[:S]),
            "offs3": striped(perm[:P]), "offs4": striped(perm[P:2 * P]),
            "w4_words": w4_words, "w4_scales": w4_scales, "base": base}

def reference(tab_words, tab_scales, offs, w1, fit, gain, wgs, page0,
              offs2, offs3, offs4, w4_words, w4_scales, base):
    v = unpack_weight(tab_words, tab_scales, "e4m3")[:, unstriped(offs)]
    w4 = unpack_weight(w4_words, w4_scales, "e2m1")
    y = mxq(f64(w1), 0, "e4m3").T @ v
    h = f64(gain)[:, None] * np.tanh(f64(fit) * y)
    page = f64(page0).copy()
    page[:, unstriped(offs2)] = np.tile(f64(wgs), (H // 128, 1)) * h
    a = page[:, unstriped(offs3)]
    b = page[:, unstriped(offs4)]
    page[:, unstriped(offs3)] = np.abs(a - b)
    page[:, unstriped(offs4)] = a + b
    return (w4.T @ mxq(page, 0, "e4m3")) + f64(base)[:, None]

@@ -1,0 +1,344 @@
+from contextlib import ExitStack
+
+import concourse.mybir as mybir
+
+K, T, S, H, T2, PAIRS, N = 1536, 4096, 1024, 1024, 2048, 512, 384
+FLOPS = 2 * K * H * S + 2 * H * N * T2
+
+F32 = mybir.dt.float32
+BF16 = mybir.dt.bfloat16
+I32 = mybir.dt.int32
+U32 = mybir.dt.uint32
+U16 = mybir.dt.uint16
+U8 = mybir.dt.uint8
+FP8X4 = mybir.dt.float8_e4m3fn_x4
+FP4X4 = mybir.dt.float4_e2m1fn_x4
+ALU = mybir.AluOpType
+ACT = mybir.ActivationFunctionType
+
+P = 128
+PACK = 4
+K_PASS = P * PACK
+BANK = 512
+K_PASSES = K // K_PASS
+R_PASSES = H // K_PASS
+SLICES = R_PASSES * PACK
+CHUNKS = T2 // BANK
+M_TILES = N // P
+GROUPS = CHUNKS * M_TILES
+BANKS = 8
+
+
+def slice_rows(s):
+    return s // PACK, (0, 2, 1, 3)[s % PACK]
+
+
+def tile_list_driveway_space_ledger_kernel(
+    tc, tab_words, tab_scales, offs, w1, fit, gain, wgs, page0,
+    offs2, offs3, offs4, w4_words, w4_scales, base, out,
+):
+    nc = tc.nc
+    with ExitStack() as ctx:
+        keep = ctx.enter_context(tc.tile_pool(name="keep", bufs=1))
+        work = ctx.enter_context(tc.tile_pool(name="work", bufs=2))
+        psum = ctx.enter_context(tc.psum_pool(name="psum", bufs=1))
+
+        def load_list(source, name):
+            listed = keep.tile(list(source.shape), U16, name=name)
+            nc.sync.dma_start(listed[:], source)
+            return listed
+
+        banks = [psum.tile([P, BANK], F32, name="bank%d" % i) for i in range(BANKS)]
+        woven = [keep.tile([P, BANK * PACK], BF16, name="woven%d" % c, align_bytes=64) for c in range(CHUNKS)]
+        h_ring = [keep.tile([P, S], F32, name="h%d" % i) for i in range(3)]
+        weighed_ring = [keep.tile([P, S], F32, name="weighed%d" % i) for i in range(2)]
+
+        w1_codes, w1_scales = {}, {}
+        w1_raw = {}
+
+        def load_w1(a, b):
+            raw = work.tile([P, PACK, K_PASS], F32, name="w1_raw", bufs=3)
+            rows = w1[K_PASS * a : K_PASS * (a + 1), K_PASS * b : K_PASS * (b + 1)]
+            nc.sync.dma_start(raw[:], rows.rearrange("(p j) c -> p j c", j=PACK))
+            w1_raw[a, b] = raw
+
+        def quantise_w1(a, b, copy):
+            grouped = woven[a] if b == 0 else late.tile([P, K_PASS * PACK], BF16, name="grouped%d" % a, align_bytes=64)
+            copy(
+                grouped[:].rearrange("p (t m j) -> p m j t", t=PACK, j=PACK),
+                w1_raw[a, b][:].rearrange("p j (m t) -> p m j t", t=PACK),
+            )
+            codes = keep.tile([P, K_PASS], U32, name="w1_codes%d%d" % (a, b), align_bytes=64)
+            scales = keep.tile([P, K_PASS], U8, name="w1_scales%d%d" % (a, b), align_bytes=64)
+            nc.vector.quantize_mx(out=codes[:].bitcast(FP8X4), scales=scales[:], in_=grouped[:])
+            w1_codes[a, b], w1_scales[a, b] = codes, scales
+
+        fit_rows = fit.rearrange("(b p t) j -> b t p j", p=P, t=PACK)
+        page_rows = page0.rearrange("(b p t) c -> b t p c", p=P, t=PACK)
+        wgs_rows = wgs.rearrange("(m t) j -> t m j", t=PACK)
+        fits, pages, dealt, hs = {}, {}, {}, {}
+
+        def load_fit(s):
+            fits[s] = work.tile([P, S], F32, name="fit_tile", bufs=3)
+            nc.sync.dma_start(fits[s][:], fit_rows[slice_rows(s)])
+
+        def load_page(s):
+            tile = work.tile([P, T2], F32, name="page", bufs=4)
+            nc.sync.dma_start(tile[:], page_rows[slice_rows(s)])
+            pages[s] = tile
+
+        def load_wgs(s):
+            dealt[s] = keep.tile([P, S], F32, name="dealt%d" % s)
+            for q in range(4):
+                nc.sync.dma_start(dealt[s][32 * q : 32 * (q + 1), :], wgs_rows[slice_rows(s)[1]])
+
+        picked = [keep.tile([P, S], U32, name="picked%d" % a, align_bytes=64) for a in range(K_PASSES)]
+        picked_scales = keep.tile([P, S], U8, name="picked_scales", align_bytes=64)
+
+        with tc.tile_pool(name="table", bufs=1) as table:
+            load_w1(0, 0)
+            list1 = load_list(offs, "list1")
+            list2 = load_list(offs2, "list2")
+            list3 = load_list(offs3, "list3")
+            list4 = load_list(offs4, "list4")
+            gains = keep.tile([P, R_PASSES, PACK], F32, name="gains")
+            nc.sync.dma_start(gains[:], gain.rearrange("(b p t) -> p b t", p=P, t=PACK))
+            scale_rows = table.tile([P, T], U8, name="scale_rows")
+            nc.vector.memset(scale_rows[:].bitcast(I32), 0)
+            words = []
+            for a in range(K_PASSES):
+                if a > 0:
+                    load_w1(a, 0)
+                if a == 1:
+                    for q in range(4):
+                        nc.sync.dma_start(
+                            scale_rows[32 * q : 32 * q + 4 * K_PASSES, :].bitcast(I32),
+                            tab_scales[:, 4 * q : 4 * q + 4, :].bitcast(I32),
+                        )
+                tile = table.tile([P, T], U32, name="words%d" % a)
+                nc.sync.dma_start(
+                    tile[:].bitcast(I32), tab_words[a].rearrange("p t i -> p (t i)").bitcast(I32)
+                )
+                words.append(tile)
+            for a in range(K_PASSES):
+                quantise_w1(a, 0, nc.vector.tensor_copy)
+                if a == 1:
+                    nc.vector.tensor_copy(picked_scales[:], scale_rows[:].indirect(list1[:]))
+                parts = 2 if a == K_PASSES - 1 else 1
+                width = S // parts
+                for i in range(parts):
+                    nc.vector.tensor_copy(
+                        picked[a][:, width * i : width * (i + 1)],
+                        words[a][:].indirect(list1[:, width // 16 * i : width // 16 * (i + 1)]),
+                    )
+
+        late = ctx.enter_context(tc.tile_pool(name="late", bufs=1))
+
+        load_wgs(0)
+        load_fit(0)
+        load_fit(1)
+        load_page(0)
+        load_wgs(1)
+        load_page(1)
+        load_page(2)
+        load_wgs(2)
+        load_fit(2)
+        for a in range(K_PASSES):
+            load_w1(a, 1)
+
+        def gain_of(s):
+            b, t = slice_rows(s)
+            return gains[:, b, t : t + 1]
+
+        def features(s):
+            b, t = slice_rows(s)
+            h = h_ring[s % 3]
+            for half in range(S // BANK):
+                cols = slice(BANK * half, BANK * (half + 1))
+                acc = banks[2 * (s % 2) + half]
+                for a in range(K_PASSES):
+                    nc.tensor.matmul_mx(
+                        out=acc[:],
+                        lhsT=w1_codes[a, b][:, P * t : P * (t + 1)].bitcast(FP8X4),
+                        lhsT_scale=w1_scales[a, b][:, P * t : P * (t + 1)],
+                        rhs=picked[a][:, cols].bitcast(FP8X4),
+                        rhs_scale=picked_scales[4 * a : P, cols],
+                        start=(a == 0),
+                        stop=(a == K_PASSES - 1),
+                    )
+                if s < 2:
+                    nc.vector.tensor_tensor(h[:, cols], acc[:], fits[s][:, cols], ALU.mult)
+                    nc.scalar.activation(h[:, cols], h[:, cols], ACT.Tanh)
+                else:
+                    nc.scalar.copy(h[:, cols], acc[:])
+            if s >= 2:
+                nc.gpsimd.tensor_tensor(h[:], h[:], fits[s][:], ALU.mult)
+                nc.scalar.activation(h[:], h[:], ACT.Tanh)
+            if s >= 1:
+                nc.scalar.activation(h[:], h[:], ACT.Copy, scale=gain_of(s))
+            hs[s] = h
+
+        def put_requests(s):
+            if s == 0:
+                nc.vector.tensor_tensor(pages[s][:].indirect(list2[:]), hs[s][:], h_ring[2][:], ALU.mult)
+            else:
+                nc.vector.tensor_copy(pages[s][:].indirect(list2[:]), weighed_ring[s % 2][:])
+
+        fetched = {}
+
+        def fetch_pairs(s):
+            first = work.tile([P, PAIRS], F32, name="first", bufs=1)
+            second = work.tile([P, PAIRS], F32, name="second", bufs=1)
+            nc.vector.tensor_copy(first[:], pages[s][:].indirect(list3[:]))
+            nc.vector.tensor_copy(second[:], pages[s][:].indirect(list4[:]))
+            fetched[s] = (first, second)
+
+        combined = {}
+
+        def combine(s):
+            first, second = fetched[s]
+            if s + 1 < SLICES:
+                both = hs[s + 1]
+                nc.gpsimd.tensor_tensor(both[:, :PAIRS], first[:], second[:], ALU.add)
+                nc.gpsimd.tensor_tensor(both[:, PAIRS:], first[:], second[:], ALU.subtract)
+            else:
+                both = weighed_ring[s % 2]
+                nc.gpsimd.tensor_tensor(both[:, :PAIRS], first[:], second[:], ALU.subtract)
+                nc.gpsimd.tensor_scalar(both[:, PAIRS:], both[:, :PAIRS], -1.0, 0.0, ALU.mult, ALU.max)
+                nc.gpsimd.tensor_scalar(both[:, :PAIRS], both[:, :PAIRS], 1.0, 0.0, ALU.mult, ALU.max)
+            combined[s] = both
+
+        def put_sums(s):
+            if s + 1 < SLICES:
+                nc.vector.tensor_copy(pages[s][:].indirect(list4[:]), combined[s][:, :PAIRS])
+            else:
+                nc.vector.tensor_tensor(pages[s][:].indirect(list4[:]), fetched[s][0][:], fetched[s][1][:], ALU.add)
+
+        def put_gaps(s):
+            if s + 1 < SLICES:
+                size = fits[s + 2][:, :PAIRS] if s + 2 < SLICES else combined[s][:, PAIRS:]
+                nc.scalar.activation(size, combined[s][:, PAIRS:], ACT.Abs)
+                nc.vector.tensor_copy(pages[s][:].indirect(list3[:]), size)
+            else:
+                nc.vector.tensor_tensor(
+                    pages[s][:].indirect(list3[:]), combined[s][:, :PAIRS], combined[s][:, PAIRS:], ALU.add
+                )
+
+        def round_page(s, c, copy):
+            b, t = slice_rows(s)
+            copy(woven[c][:].rearrange("p (n t) -> p n t", t=PACK)[:, :, t], pages[s][:, BANK * c : BANK * (c + 1)])
+
+        b_codes, b_scales = {}, {}
+
+        def quantise_page(b, c):
+            codes = keep.tile([P, BANK], U32, name="b_codes%d%d" % (b, c), align_bytes=64)
+            scales = keep.tile([P, BANK], U8, name="b_scales%d%d" % (b, c), align_bytes=64)
+            nc.vector.quantize_mx(
+                out=codes[:].bitcast(FP8X4), scales=scales[:],
+                in_=woven[c][:],
+            )
+            b_codes[b, c], b_scales[b, c] = codes, scales
+
+        w4_codes = keep.tile([P, R_PASSES, 2 * N], U8, name="w4_codes", align_bytes=64)
+        w4_planes = keep.tile([P, R_PASSES, N], U8, name="w4_planes", align_bytes=64)
+        bases = keep.tile([P, M_TILES], F32, name="bases")
+
+        def load_w4():
+            nc.vector.memset(w4_planes[:].bitcast(I32), 0)
+            nc.sync.dma_start(w4_codes[:].bitcast(I32), w4_words.rearrange("a p c -> p a c").bitcast(I32))
+            for q in range(4):
+                nc.sync.dma_start(
+                    w4_planes[32 * q : 32 * q + 4, :, :].bitcast(I32),
+                    w4_scales[:, 4 * q : 4 * q + 4, :].rearrange("a r n -> r a n").bitcast(I32),
+                )
+            with nc.allow_non_contiguous_dma(reason="one bias value a partition"):
+                nc.sync.dma_start(bases[:], base.rearrange("(m p) -> p m", p=P))
+
+        def allocate(acc, g, b, start, stop):
+            c, m = divmod(g, M_TILES)
+            nc.tensor.matmul_mx(
+                out=acc[:],
+                lhsT=w4_codes[:, b, 2 * P * m : 2 * P * (m + 1)].bitcast(FP4X4),
+                lhsT_scale=w4_planes[:, b, P * m : P * (m + 1)],
+                rhs=b_codes[b, c][:].bitcast(FP8X4),
+                rhs_scale=b_scales[b, c][:],
+                start=start,
+                stop=stop,
+            )
+
+        def add_base(result, acc, g):
+            m = g % M_TILES
+            nc.scalar.activation(result[:], acc[:], ACT.Identity, bias=bases[:, m : m + 1])
+
+        open_groups, parked = {}, {}
+
+        nc.scalar.activation(h_ring[2][:], dealt[0][:], ACT.Copy, scale=gain_of(0))
+        features(0)
+        def weigh(s):
+            nc.gpsimd.tensor_tensor(weighed_ring[s % 2][:], hs[s][:], dealt[s % PACK][:], ALU.mult)
+
+        features(1)
+        put_requests(0)
+        fetch_pairs(0)
+        weigh(1)
+        put_requests(1)
+        combine(0)
+        put_sums(0)
+        fetch_pairs(1)
+        for a in range(K_PASSES):
+            quantise_w1(a, 1, nc.scalar.copy)
+        for s in range(SLICES):
+            if s + 3 < SLICES:
+                load_page(s + 3)
+                if s + 3 < PACK:
+                    load_wgs(s + 3)
+                load_fit(s + 3)
+            if s == 1:
+                load_w4()
+            if s + 2 < SLICES:
+                features(s + 2)
+            put_gaps(s)
+            if s + 2 < SLICES:
+                weigh(s + 2)
+                put_requests(s + 2)
+            if s + 1 < SLICES:
+                combine(s + 1)
+                put_sums(s + 1)
+            if s + 2 < SLICES:
+                fetch_pairs(s + 2)
+            if s + 1 < SLICES:
+                for c in range(CHUNKS):
+                    round_page(s, c, nc.scalar.copy)
+            if s == PACK - 1:
+                for c in range(CHUNKS):
+                    quantise_page(0, c)
+            if s == PACK:
+                for g in range(4):
+                    open_groups[g] = banks[4 + g]
+                    allocate(open_groups[g], BANKS + g, 0, True, True)
+                    parked[BANKS + g] = late.tile([P, BANK], F32, name="parked%d" % g)
+                    add_base(parked[BANKS + g], open_groups[g], BANKS + g)
+                for g in range(4):
+                    allocate(open_groups[g], g, 0, True, False)
+        for g in range(4, BANKS):
+            open_groups[g] = banks[g - 4]
+            allocate(open_groups[g], g, 0, True, False)
+
+        last = SLICES - 1
+        round_page(last, CHUNKS - 1, nc.scalar.copy)
+        round_page(last, 0, nc.vector.tensor_copy)
+        for c in range(CHUNKS):
+            if c + 1 < CHUNKS - 1:
+                round_page(last, c + 1, nc.vector.tensor_copy)
+            quantise_page(1, c)
+        for g in range(GROUPS):
+            c, m = divmod(g, M_TILES)
+            result = late.tile([P, BANK], F32, name="result%d" % g)
+            if g < BANKS:
+                allocate(open_groups[g], g, 1, False, True)
+                add_base(result, open_groups[g], g)
+            else:
+                acc = open_groups[g - BANKS]
+                allocate(acc, g, 1, True, True)
+                nc.vector.tensor_tensor(result[:], acc[:], parked[g][:], ALU.add)
+            nc.sync.dma_start(out[P * m : P * (m + 1), BANK * c : BANK * (c + 1)], result[:])

@@ -27,6 +27,7 @@ CHUNKS = T2 // BANK
 M_TILES = N // P
 GROUPS = CHUNKS * M_TILES
 BANKS = 8
+QUADRANTS = (0, 2, 1, 3)
 
 
 def slice_rows(s):
@@ -50,7 +51,7 @@ def tile_list_driveway_space_ledger_kernel(
 
         banks = [psum.tile([P, BANK], F32, name="bank%d" % i) for i in range(BANKS)]
         woven = [keep.tile([P, BANK * PACK], BF16, name="woven%d" % c, align_bytes=64) for c in range(CHUNKS)]
-        h_ring = [keep.tile([P, S], F32, name="h%d" % i) for i in range(3)]
+        spare = keep.tile([P, S], F32, name="spare")
         weighed_ring = [keep.tile([P, S], F32, name="weighed%d" % i) for i in range(2)]
 
         w1_codes, w1_scales = {}, {}
@@ -65,8 +66,8 @@ def tile_list_driveway_space_ledger_kernel(
         def quantise_w1(a, b, copy):
             grouped = woven[a] if b == 0 else late.tile([P, K_PASS * PACK], BF16, name="grouped%d" % a, align_bytes=64)
             copy(
-                grouped[:].rearrange("p (t m j) -> p m j t", t=PACK, j=PACK),
-                w1_raw[a, b][:].rearrange("p j (m t) -> p m j t", t=PACK),
+                grouped[:].rearrange("p (t m j) -> p t m j", t=PACK, j=PACK),
+                w1_raw[a, b][:].rearrange("p j (m t) -> p t m j", t=PACK),
             )
             codes = keep.tile([P, K_PASS], U32, name="w1_codes%d%d" % (a, b), align_bytes=64)
             scales = keep.tile([P, K_PASS], U8, name="w1_scales%d%d" % (a, b), align_bytes=64)
@@ -76,10 +77,10 @@ def tile_list_driveway_space_ledger_kernel(
         fit_rows = fit.rearrange("(b p t) j -> b t p j", p=P, t=PACK)
         page_rows = page0.rearrange("(b p t) c -> b t p c", p=P, t=PACK)
         wgs_rows = wgs.rearrange("(m t) j -> t m j", t=PACK)
-        fits, pages, dealt, hs = {}, {}, {}, {}
+        fits, pages, dealt = {}, {}, {}
 
         def load_fit(s):
-            fits[s] = work.tile([P, S], F32, name="fit_tile", bufs=3)
+            fits[s] = work.tile([P, S], F32, name="fit_tile", bufs=4)
             nc.sync.dma_start(fits[s][:], fit_rows[slice_rows(s)])
 
         def load_page(s):
@@ -89,7 +90,7 @@ def tile_list_driveway_space_ledger_kernel(
 
         def load_wgs(s):
             dealt[s] = keep.tile([P, S], F32, name="dealt%d" % s)
-            for q in range(4):
+            for q in QUADRANTS:
                 nc.sync.dma_start(dealt[s][32 * q : 32 * (q + 1), :], wgs_rows[slice_rows(s)[1]])
 
         picked = [keep.tile([P, S], U32, name="picked%d" % a, align_bytes=64) for a in range(K_PASSES)]
@@ -110,7 +111,7 @@ def tile_list_driveway_space_ledger_kernel(
                 if a > 0:
                     load_w1(a, 0)
                 if a == 1:
-                    for q in range(4):
+                    for q in QUADRANTS:
                         nc.sync.dma_start(
                             scale_rows[32 * q : 32 * q + 4 * K_PASSES, :].bitcast(I32),
                             tab_scales[:, 4 * q : 4 * q + 4, :].bitcast(I32),
@@ -121,7 +122,7 @@ def tile_list_driveway_space_ledger_kernel(
                 )
                 words.append(tile)
             for a in range(K_PASSES):
-                quantise_w1(a, 0, nc.vector.tensor_copy)
+                quantise_w1(a, 0, nc.vector.tensor_copy if a == K_PASSES - 1 else nc.scalar.copy)
                 if a == 1:
                     nc.vector.tensor_copy(picked_scales[:], scale_rows[:].indirect(list1[:]))
                 parts = 2 if a == K_PASSES - 1 else 1
@@ -138,13 +139,13 @@ def tile_list_driveway_space_ledger_kernel(
         load_fit(0)
         load_fit(1)
         load_page(0)
-        load_wgs(1)
         load_page(1)
+        load_wgs(1)
+        for a in range(K_PASSES):
+            load_w1(a, 1)
         load_page(2)
         load_wgs(2)
         load_fit(2)
-        for a in range(K_PASSES):
-            load_w1(a, 1)
 
         def gain_of(s):
             b, t = slice_rows(s)
@@ -152,7 +153,7 @@ def tile_list_driveway_space_ledger_kernel(
 
         def features(s):
             b, t = slice_rows(s)
-            h = h_ring[s % 3]
+            h = fits[s]
             for half in range(S // BANK):
                 cols = slice(BANK * half, BANK * (half + 1))
                 acc = banks[2 * (s % 2) + half]
@@ -167,20 +168,22 @@ def tile_list_driveway_space_ledger_kernel(
                         stop=(a == K_PASSES - 1),
                     )
                 if s < 2:
-                    nc.vector.tensor_tensor(h[:, cols], acc[:], fits[s][:, cols], ALU.mult)
+                    nc.vector.tensor_tensor(h[:, cols], acc[:], h[:, cols], ALU.mult)
                     nc.scalar.activation(h[:, cols], h[:, cols], ACT.Tanh)
                 else:
-                    nc.scalar.copy(h[:, cols], acc[:])
-            if s >= 2:
-                nc.gpsimd.tensor_tensor(h[:], h[:], fits[s][:], ALU.mult)
-                nc.scalar.activation(h[:], h[:], ACT.Tanh)
-            if s >= 1:
+                    nc.scalar.copy(spare[:, cols], acc[:])
+                    nc.gpsimd.tensor_tensor(h[:, cols], spare[:, cols], h[:, cols], ALU.mult)
+            if s == 1:
                 nc.scalar.activation(h[:], h[:], ACT.Copy, scale=gain_of(s))
-            hs[s] = h
+            if s >= 2:
+                for half in range(S // BANK):
+                    cols = slice(BANK * half, BANK * (half + 1))
+                    nc.scalar.activation(spare[:, cols], h[:, cols], ACT.Tanh)
+                    nc.gpsimd.tensor_scalar(h[:, cols], spare[:, cols], gain_of(s), 0.0, ALU.mult, ALU.add)
 
         def put_requests(s):
             if s == 0:
-                nc.vector.tensor_tensor(pages[s][:].indirect(list2[:]), hs[s][:], h_ring[2][:], ALU.mult)
+                nc.vector.tensor_tensor(pages[s][:].indirect(list2[:]), fits[s][:], weighed_ring[0][:], ALU.mult)
             else:
                 nc.vector.tensor_copy(pages[s][:].indirect(list2[:]), weighed_ring[s % 2][:])
 
@@ -193,36 +196,24 @@ def tile_list_driveway_space_ledger_kernel(
             nc.vector.tensor_copy(second[:], pages[s][:].indirect(list4[:]))
             fetched[s] = (first, second)
 
-        combined = {}
+        combined, sizes = {}, {}
 
         def combine(s):
             first, second = fetched[s]
-            if s + 1 < SLICES:
-                both = hs[s + 1]
-                nc.gpsimd.tensor_tensor(both[:, :PAIRS], first[:], second[:], ALU.add)
-                nc.gpsimd.tensor_tensor(both[:, PAIRS:], first[:], second[:], ALU.subtract)
-            else:
-                both = weighed_ring[s % 2]
-                nc.gpsimd.tensor_tensor(both[:, :PAIRS], first[:], second[:], ALU.subtract)
-                nc.gpsimd.tensor_scalar(both[:, PAIRS:], both[:, :PAIRS], -1.0, 0.0, ALU.mult, ALU.max)
-                nc.gpsimd.tensor_scalar(both[:, :PAIRS], both[:, :PAIRS], 1.0, 0.0, ALU.mult, ALU.max)
+            both = fits[s + 1] if s + 1 < SLICES else weighed_ring[s % 2]
+            nc.gpsimd.tensor_tensor(both[:, :PAIRS], first[:], second[:], ALU.add)
+            nc.gpsimd.tensor_tensor(both[:, PAIRS:], first[:], second[:], ALU.subtract)
             combined[s] = both
 
         def put_sums(s):
-            if s + 1 < SLICES:
-                nc.vector.tensor_copy(pages[s][:].indirect(list4[:]), combined[s][:, :PAIRS])
-            else:
-                nc.vector.tensor_tensor(pages[s][:].indirect(list4[:]), fetched[s][0][:], fetched[s][1][:], ALU.add)
+            nc.vector.tensor_copy(pages[s][:].indirect(list4[:]), combined[s][:, :PAIRS])
+
+        def take_size(s):
+            sizes[s] = spare[:, PAIRS // 2 : PAIRS // 2 + PAIRS] if s + 2 < SLICES else combined[s][:, PAIRS:]
+            nc.scalar.activation(sizes[s], combined[s][:, PAIRS:], ACT.Abs)
 
         def put_gaps(s):
-            if s + 1 < SLICES:
-                size = fits[s + 2][:, :PAIRS] if s + 2 < SLICES else combined[s][:, PAIRS:]
-                nc.scalar.activation(size, combined[s][:, PAIRS:], ACT.Abs)
-                nc.vector.tensor_copy(pages[s][:].indirect(list3[:]), size)
-            else:
-                nc.vector.tensor_tensor(
-                    pages[s][:].indirect(list3[:]), combined[s][:, :PAIRS], combined[s][:, PAIRS:], ALU.add
-                )
+            nc.vector.tensor_copy(pages[s][:].indirect(list3[:]), sizes[s])
 
         def round_page(s, c, copy):
             b, t = slice_rows(s)
@@ -268,14 +259,14 @@ def tile_list_driveway_space_ledger_kernel(
 
         def add_base(result, acc, g):
             m = g % M_TILES
-            nc.scalar.activation(result[:], acc[:], ACT.Identity, bias=bases[:, m : m + 1])
+            nc.scalar.activation(result, acc[:], ACT.Identity, bias=bases[:, m : m + 1])
 
-        open_groups, parked = {}, {}
+        parked = {}
 
-        nc.scalar.activation(h_ring[2][:], dealt[0][:], ACT.Copy, scale=gain_of(0))
+        nc.scalar.activation(weighed_ring[0][:], dealt[0][:], ACT.Copy, scale=gain_of(0))
         features(0)
         def weigh(s):
-            nc.gpsimd.tensor_tensor(weighed_ring[s % 2][:], hs[s][:], dealt[s % PACK][:], ALU.mult)
+            nc.gpsimd.tensor_tensor(weighed_ring[s % 2][:], fits[s][:], dealt[s % PACK][:], ALU.mult)
 
         features(1)
         put_requests(0)
@@ -287,6 +278,8 @@ def tile_list_driveway_space_ledger_kernel(
         fetch_pairs(1)
         for a in range(K_PASSES):
             quantise_w1(a, 1, nc.scalar.copy)
+        features(2)
+        take_size(0)
         for s in range(SLICES):
             if s + 3 < SLICES:
                 load_page(s + 3)
@@ -295,8 +288,6 @@ def tile_list_driveway_space_ledger_kernel(
                 load_fit(s + 3)
             if s == 1:
                 load_w4()
-            if s + 2 < SLICES:
-                features(s + 2)
             put_gaps(s)
             if s + 2 < SLICES:
                 weigh(s + 2)
@@ -306,7 +297,10 @@ def tile_list_driveway_space_ledger_kernel(
                 put_sums(s + 1)
             if s + 2 < SLICES:
                 fetch_pairs(s + 2)
+            if s + 3 < SLICES:
+                features(s + 3)
             if s + 1 < SLICES:
+                take_size(s + 1)
                 for c in range(CHUNKS):
                     round_page(s, c, nc.scalar.copy)
             if s == PACK - 1:
@@ -314,15 +308,13 @@ def tile_list_driveway_space_ledger_kernel(
                     quantise_page(0, c)
             if s == PACK:
                 for g in range(4):
-                    open_groups[g] = banks[4 + g]
-                    allocate(open_groups[g], BANKS + g, 0, True, True)
-                    parked[BANKS + g] = late.tile([P, BANK], F32, name="parked%d" % g)
-                    add_base(parked[BANKS + g], open_groups[g], BANKS + g)
+                    allocate(banks[4 + g], g, 0, True, False)
+            if s == PACK + 1:
                 for g in range(4):
-                    allocate(open_groups[g], g, 0, True, False)
-        for g in range(4, BANKS):
-            open_groups[g] = banks[g - 4]
-            allocate(open_groups[g], g, 0, True, False)
+                    allocate(banks[g], BANKS + g, 0, True, True)
+                    parked[BANKS + g] = (weighed_ring[0], spare)[g // 2][:, BANK * (g % 2) : BANK * (g % 2 + 1)]
+                    add_base(parked[BANKS + g], banks[g], BANKS + g)
+                    allocate(banks[g], 4 + g, 0, True, False)
 
         last = SLICES - 1
         round_page(last, CHUNKS - 1, nc.scalar.copy)
@@ -334,11 +326,11 @@ def tile_list_driveway_space_ledger_kernel(
         for g in range(GROUPS):
             c, m = divmod(g, M_TILES)
             result = late.tile([P, BANK], F32, name="result%d" % g)
+            acc = banks[(g + 4) % BANKS]
             if g < BANKS:
-                allocate(open_groups[g], g, 1, False, True)
-                add_base(result, open_groups[g], g)
+                allocate(acc, g, 1, False, True)
+                add_base(result[:], acc, g)
             else:
-                acc = open_groups[g - BANKS]
                 allocate(acc, g, 1, True, True)
-                nc.vector.tensor_tensor(result[:], acc[:], parked[g][:], ALU.add)
+                nc.vector.tensor_tensor(result[:], acc[:], parked[g], ALU.add)
             nc.sync.dma_start(out[P * m : P * (m + 1), BANK * c : BANK * (c + 1)], result[:])

@@ -20,18 +20,26 @@ P = 128
 PACK = 4
 K_PASS = P * PACK
 BANK = 512
+BANKS = 8
+LIST_ROWS = 16
+QUAD = 32
+SCALE_ROWS = 4
 K_PASSES = K // K_PASS
 R_PASSES = H // K_PASS
 SLICES = R_PASSES * PACK
 CHUNKS = T2 // BANK
 M_TILES = N // P
 GROUPS = CHUNKS * M_TILES
-BANKS = 8
+HALF_BANKS = BANKS // 2
+
 QUADRANTS = (0, 2, 1, 3)
+T_ORDER = (0, 2, 1, 3)
+W1_BUFS, PAGE_BUFS, FIT_BUFS = K_PASSES, 4, 4
+VECTOR_SLICES = 2
 
 
 def slice_rows(s):
-    return s // PACK, (0, 2, 1, 3)[s % PACK]
+    return s // PACK, T_ORDER[s % PACK]
 
 
 def tile_list_driveway_space_ledger_kernel(
@@ -52,26 +60,24 @@ def tile_list_driveway_space_ledger_kernel(
         banks = [psum.tile([P, BANK], F32, name="bank%d" % i) for i in range(BANKS)]
         woven = [keep.tile([P, BANK * PACK], BF16, name="woven%d" % c, align_bytes=64) for c in range(CHUNKS)]
         spare = keep.tile([P, S], F32, name="spare")
-        weighed_ring = [keep.tile([P, S], F32, name="weighed%d" % i) for i in range(2)]
+        weighed = [keep.tile([P, S], F32, name="weighed%d" % i, align_bytes=64) for i in range(2)]
 
-        w1_codes, w1_scales = {}, {}
-        w1_raw = {}
+        w1_raw, w1_codes, w1_scales = {}, {}, {}
 
         def load_w1(a, b):
-            raw = work.tile([P, PACK, K_PASS], F32, name="w1_raw", bufs=3)
+            raw = work.tile([P, PACK, K_PASS], F32, name="w1_raw", bufs=W1_BUFS)
             rows = w1[K_PASS * a : K_PASS * (a + 1), K_PASS * b : K_PASS * (b + 1)]
             nc.sync.dma_start(raw[:], rows.rearrange("(p j) c -> p j c", j=PACK))
             w1_raw[a, b] = raw
 
-        def quantise_w1(a, b, copy):
-            grouped = woven[a] if b == 0 else late.tile([P, K_PASS * PACK], BF16, name="grouped%d" % a, align_bytes=64)
+        def quantise_w1(a, b, copy, grouped):
             copy(
-                grouped[:].rearrange("p (t m j) -> p t m j", t=PACK, j=PACK),
+                grouped.rearrange("p (t m j) -> p t m j", t=PACK, j=PACK),
                 w1_raw[a, b][:].rearrange("p j (m t) -> p t m j", t=PACK),
             )
             codes = keep.tile([P, K_PASS], U32, name="w1_codes%d%d" % (a, b), align_bytes=64)
             scales = keep.tile([P, K_PASS], U8, name="w1_scales%d%d" % (a, b), align_bytes=64)
-            nc.vector.quantize_mx(out=codes[:].bitcast(FP8X4), scales=scales[:], in_=grouped[:])
+            nc.vector.quantize_mx(out=codes[:].bitcast(FP8X4), scales=scales[:], in_=grouped)
             w1_codes[a, b], w1_scales[a, b] = codes, scales
 
         fit_rows = fit.rearrange("(b p t) j -> b t p j", p=P, t=PACK)
@@ -80,18 +86,17 @@ def tile_list_driveway_space_ledger_kernel(
         fits, pages, dealt = {}, {}, {}
 
         def load_fit(s):
-            fits[s] = work.tile([P, S], F32, name="fit_tile", bufs=4)
+            fits[s] = work.tile([P, S], F32, name="fit_tile", bufs=FIT_BUFS)
             nc.sync.dma_start(fits[s][:], fit_rows[slice_rows(s)])
 
         def load_page(s):
-            tile = work.tile([P, T2], F32, name="page", bufs=4)
-            nc.sync.dma_start(tile[:], page_rows[slice_rows(s)])
-            pages[s] = tile
+            pages[s] = work.tile([P, T2], F32, name="page", bufs=PAGE_BUFS)
+            nc.sync.dma_start(pages[s][:], page_rows[slice_rows(s)])
 
         def load_wgs(s):
             dealt[s] = keep.tile([P, S], F32, name="dealt%d" % s)
             for q in QUADRANTS:
-                nc.sync.dma_start(dealt[s][32 * q : 32 * (q + 1), :], wgs_rows[slice_rows(s)[1]])
+                nc.sync.dma_start(dealt[s][QUAD * q : QUAD * (q + 1), :], wgs_rows[slice_rows(s)[1]])
 
         picked = [keep.tile([P, S], U32, name="picked%d" % a, align_bytes=64) for a in range(K_PASSES)]
         picked_scales = keep.tile([P, S], U8, name="picked_scales", align_bytes=64)
@@ -104,6 +109,7 @@ def tile_list_driveway_space_ledger_kernel(
             list4 = load_list(offs4, "list4")
             gains = keep.tile([P, R_PASSES, PACK], F32, name="gains")
             nc.sync.dma_start(gains[:], gain.rearrange("(b p t) -> p b t", p=P, t=PACK))
+
             scale_rows = table.tile([P, T], U8, name="scale_rows")
             nc.vector.memset(scale_rows[:].bitcast(I32), 0)
             words = []
@@ -112,25 +118,23 @@ def tile_list_driveway_space_ledger_kernel(
                     load_w1(a, 0)
                 if a == 1:
                     for q in QUADRANTS:
-                        nc.sync.dma_start(
-                            scale_rows[32 * q : 32 * q + 4 * K_PASSES, :].bitcast(I32),
-                            tab_scales[:, 4 * q : 4 * q + 4, :].bitcast(I32),
+                        nc.gpsimd.dma_start(
+                            scale_rows[QUAD * q : QUAD * q + SCALE_ROWS * K_PASSES, :].bitcast(I32),
+                            tab_scales[:, SCALE_ROWS * q : SCALE_ROWS * (q + 1), :].bitcast(I32),
                         )
-                tile = table.tile([P, T], U32, name="words%d" % a)
+                words.append(table.tile([P, T], U32, name="words%d" % a))
                 nc.sync.dma_start(
-                    tile[:].bitcast(I32), tab_words[a].rearrange("p t i -> p (t i)").bitcast(I32)
+                    words[a][:].bitcast(I32), tab_words[a].rearrange("p t i -> p (t i)").bitcast(I32)
                 )
-                words.append(tile)
             for a in range(K_PASSES):
-                quantise_w1(a, 0, nc.vector.tensor_copy if a == K_PASSES - 1 else nc.scalar.copy)
+                quantise_w1(a, 0, nc.scalar.copy if a == 1 else nc.vector.tensor_copy, woven[a][:])
                 if a == 1:
                     nc.vector.tensor_copy(picked_scales[:], scale_rows[:].indirect(list1[:]))
-                parts = 2 if a == K_PASSES - 1 else 1
-                width = S // parts
-                for i in range(parts):
+                width = BANK if a == K_PASSES - 1 else S
+                for j0 in range(0, S, width):
                     nc.vector.tensor_copy(
-                        picked[a][:, width * i : width * (i + 1)],
-                        words[a][:].indirect(list1[:, width // 16 * i : width // 16 * (i + 1)]),
+                        picked[a][:, j0 : j0 + width],
+                        words[a][:].indirect(list1[:, j0 // LIST_ROWS : (j0 + width) // LIST_ROWS]),
                     )
 
         late = ctx.enter_context(tc.tile_pool(name="late", bufs=1))
@@ -154,40 +158,39 @@ def tile_list_driveway_space_ledger_kernel(
         def features(s):
             b, t = slice_rows(s)
             h = fits[s]
-            for half in range(S // BANK):
-                cols = slice(BANK * half, BANK * (half + 1))
-                acc = banks[2 * (s % 2) + half]
+            halves = [slice(j0, j0 + BANK) for j0 in range(0, S, BANK)]
+            for half, cols in enumerate(halves):
+                acc = banks[len(halves) * (s % 2) + half]
                 for a in range(K_PASSES):
                     nc.tensor.matmul_mx(
                         out=acc[:],
                         lhsT=w1_codes[a, b][:, P * t : P * (t + 1)].bitcast(FP8X4),
                         lhsT_scale=w1_scales[a, b][:, P * t : P * (t + 1)],
                         rhs=picked[a][:, cols].bitcast(FP8X4),
-                        rhs_scale=picked_scales[4 * a : P, cols],
+                        rhs_scale=picked_scales[SCALE_ROWS * a : P, cols],
                         start=(a == 0),
                         stop=(a == K_PASSES - 1),
                     )
-                if s < 2:
+                if s < VECTOR_SLICES:
                     nc.vector.tensor_tensor(h[:, cols], acc[:], h[:, cols], ALU.mult)
                     nc.scalar.activation(h[:, cols], h[:, cols], ACT.Tanh)
                 else:
                     nc.scalar.copy(spare[:, cols], acc[:])
                     nc.gpsimd.tensor_tensor(h[:, cols], spare[:, cols], h[:, cols], ALU.mult)
-            if s == 1:
-                nc.scalar.activation(h[:], h[:], ACT.Copy, scale=gain_of(s))
-            if s >= 2:
-                for half in range(S // BANK):
-                    cols = slice(BANK * half, BANK * (half + 1))
+            if s >= VECTOR_SLICES:
+                for cols in halves:
                     nc.scalar.activation(spare[:, cols], h[:, cols], ACT.Tanh)
                     nc.gpsimd.tensor_scalar(h[:, cols], spare[:, cols], gain_of(s), 0.0, ALU.mult, ALU.add)
+            elif s > 0:
+                nc.scalar.activation(h[:], h[:], ACT.Copy, scale=gain_of(s))
+
+        def weigh(s):
+            nc.gpsimd.tensor_tensor(weighed[s % 2][:], fits[s][:], dealt[s % PACK][:], ALU.mult)
 
         def put_requests(s):
-            if s == 0:
-                nc.vector.tensor_tensor(pages[s][:].indirect(list2[:]), fits[s][:], weighed_ring[0][:], ALU.mult)
-            else:
-                nc.vector.tensor_copy(pages[s][:].indirect(list2[:]), weighed_ring[s % 2][:])
+            nc.vector.tensor_copy(pages[s][:].indirect(list2[:]), weighed[s % 2][:])
 
-        fetched = {}
+        fetched, combined, sizes = {}, {}, {}
 
         def fetch_pairs(s):
             first = work.tile([P, PAIRS], F32, name="first", bufs=1)
@@ -196,11 +199,9 @@ def tile_list_driveway_space_ledger_kernel(
             nc.vector.tensor_copy(second[:], pages[s][:].indirect(list4[:]))
             fetched[s] = (first, second)
 
-        combined, sizes = {}, {}
-
         def combine(s):
             first, second = fetched[s]
-            both = fits[s + 1] if s + 1 < SLICES else weighed_ring[s % 2]
+            both = fits[s + 1] if s + 1 < SLICES else weighed[s % 2]
             nc.gpsimd.tensor_tensor(both[:, :PAIRS], first[:], second[:], ALU.add)
             nc.gpsimd.tensor_tensor(both[:, PAIRS:], first[:], second[:], ALU.subtract)
             combined[s] = both
@@ -208,15 +209,15 @@ def tile_list_driveway_space_ledger_kernel(
         def put_sums(s):
             nc.vector.tensor_copy(pages[s][:].indirect(list4[:]), combined[s][:, :PAIRS])
 
-        def take_size(s):
+        def take_sizes(s):
             sizes[s] = spare[:, PAIRS // 2 : PAIRS // 2 + PAIRS] if s + 2 < SLICES else combined[s][:, PAIRS:]
             nc.scalar.activation(sizes[s], combined[s][:, PAIRS:], ACT.Abs)
 
-        def put_gaps(s):
+        def put_sizes(s):
             nc.vector.tensor_copy(pages[s][:].indirect(list3[:]), sizes[s])
 
         def round_page(s, c, copy):
-            b, t = slice_rows(s)
+            t = slice_rows(s)[1]
             copy(woven[c][:].rearrange("p (n t) -> p n t", t=PACK)[:, :, t], pages[s][:, BANK * c : BANK * (c + 1)])
 
         b_codes, b_scales = {}, {}
@@ -224,10 +225,7 @@ def tile_list_driveway_space_ledger_kernel(
         def quantise_page(b, c):
             codes = keep.tile([P, BANK], U32, name="b_codes%d%d" % (b, c), align_bytes=64)
             scales = keep.tile([P, BANK], U8, name="b_scales%d%d" % (b, c), align_bytes=64)
-            nc.vector.quantize_mx(
-                out=codes[:].bitcast(FP8X4), scales=scales[:],
-                in_=woven[c][:],
-            )
+            nc.vector.quantize_mx(out=codes[:].bitcast(FP8X4), scales=scales[:], in_=woven[c][:])
             b_codes[b, c], b_scales[b, c] = codes, scales
 
         w4_codes = keep.tile([P, R_PASSES, 2 * N], U8, name="w4_codes", align_bytes=64)
@@ -237,15 +235,15 @@ def tile_list_driveway_space_ledger_kernel(
         def load_w4():
             nc.vector.memset(w4_planes[:].bitcast(I32), 0)
             nc.sync.dma_start(w4_codes[:].bitcast(I32), w4_words.rearrange("a p c -> p a c").bitcast(I32))
-            for q in range(4):
+            for q in range(P // QUAD):
                 nc.sync.dma_start(
-                    w4_planes[32 * q : 32 * q + 4, :, :].bitcast(I32),
-                    w4_scales[:, 4 * q : 4 * q + 4, :].rearrange("a r n -> r a n").bitcast(I32),
+                    w4_planes[QUAD * q : QUAD * q + SCALE_ROWS, :, :].bitcast(I32),
+                    w4_scales[:, SCALE_ROWS * q : SCALE_ROWS * (q + 1), :].rearrange("a r n -> r a n").bitcast(I32),
                 )
             with nc.allow_non_contiguous_dma(reason="one bias value a partition"):
                 nc.sync.dma_start(bases[:], base.rearrange("(m p) -> p m", p=P))
 
-        def allocate(acc, g, b, start, stop):
+        def multiply_page(acc, g, b, start, stop):
             c, m = divmod(g, M_TILES)
             nc.tensor.matmul_mx(
                 out=acc[:],
@@ -261,15 +259,10 @@ def tile_list_driveway_space_ledger_kernel(
             m = g % M_TILES
             nc.scalar.activation(result, acc[:], ACT.Identity, bias=bases[:, m : m + 1])
 
-        parked = {}
-
-        nc.scalar.activation(weighed_ring[0][:], dealt[0][:], ACT.Copy, scale=gain_of(0))
+        nc.scalar.activation(weighed[0][:], dealt[0][:], ACT.Copy, scale=gain_of(0))
         features(0)
-        def weigh(s):
-            nc.gpsimd.tensor_tensor(weighed_ring[s % 2][:], fits[s][:], dealt[s % PACK][:], ALU.mult)
-
         features(1)
-        put_requests(0)
+        nc.vector.tensor_tensor(pages[0][:].indirect(list2[:]), fits[0][:], weighed[0][:], ALU.mult)
         fetch_pairs(0)
         weigh(1)
         put_requests(1)
@@ -277,9 +270,15 @@ def tile_list_driveway_space_ledger_kernel(
         put_sums(0)
         fetch_pairs(1)
         for a in range(K_PASSES):
-            quantise_w1(a, 1, nc.scalar.copy)
+            if a + 1 < K_PASSES:
+                grouped = late.tile([P, K_PASS * PACK], BF16, name="grouped%d" % a, align_bytes=64)
+                quantise_w1(a, 1, nc.scalar.copy, grouped[:])
+            else:
+                quantise_w1(a, 1, nc.scalar.copy, weighed[0][:].bitcast(BF16))
         features(2)
-        take_size(0)
+        take_sizes(0)
+
+        parked = {}
         for s in range(SLICES):
             if s + 3 < SLICES:
                 load_page(s + 3)
@@ -288,7 +287,7 @@ def tile_list_driveway_space_ledger_kernel(
                 load_fit(s + 3)
             if s == 1:
                 load_w4()
-            put_gaps(s)
+            put_sizes(s)
             if s + 2 < SLICES:
                 weigh(s + 2)
                 put_requests(s + 2)
@@ -300,21 +299,21 @@ def tile_list_driveway_space_ledger_kernel(
             if s + 3 < SLICES:
                 features(s + 3)
             if s + 1 < SLICES:
-                take_size(s + 1)
+                take_sizes(s + 1)
                 for c in range(CHUNKS):
                     round_page(s, c, nc.scalar.copy)
             if s == PACK - 1:
                 for c in range(CHUNKS):
                     quantise_page(0, c)
             if s == PACK:
-                for g in range(4):
-                    allocate(banks[4 + g], g, 0, True, False)
+                for g in range(HALF_BANKS):
+                    multiply_page(banks[HALF_BANKS + g], g, 0, True, False)
             if s == PACK + 1:
-                for g in range(4):
-                    allocate(banks[g], BANKS + g, 0, True, True)
-                    parked[BANKS + g] = (weighed_ring[0], spare)[g // 2][:, BANK * (g % 2) : BANK * (g % 2 + 1)]
-                    add_base(parked[BANKS + g], banks[g], BANKS + g)
-                    allocate(banks[g], 4 + g, 0, True, False)
+                for i in range(GROUPS - BANKS):
+                    multiply_page(banks[i], BANKS + i, 0, True, True)
+                    parked[BANKS + i] = (weighed[0], spare)[i // 2][:, BANK * (i % 2) : BANK * (i % 2 + 1)]
+                    add_base(parked[BANKS + i], banks[i], BANKS + i)
+                    multiply_page(banks[i], HALF_BANKS + i, 0, True, False)
 
         last = SLICES - 1
         round_page(last, CHUNKS - 1, nc.scalar.copy)
@@ -326,11 +325,11 @@ def tile_list_driveway_space_ledger_kernel(
         for g in range(GROUPS):
             c, m = divmod(g, M_TILES)
             result = late.tile([P, BANK], F32, name="result%d" % g)
-            acc = banks[(g + 4) % BANKS]
+            acc = banks[(g + HALF_BANKS) % BANKS]
             if g < BANKS:
-                allocate(acc, g, 1, False, True)
+                multiply_page(acc, g, 1, False, True)
                 add_base(result[:], acc, g)
             else:
-                allocate(acc, g, 1, True, True)
+                multiply_page(acc, g, 1, True, True)
                 nc.vector.tensor_tensor(result[:], acc[:], parked[g], ALU.add)
             nc.sync.dma_start(out[P * m : P * (m + 1), BANK * c : BANK * (c + 1)], result[:])

@@ -105,8 +105,6 @@ def tile_list_driveway_space_ledger_kernel(
             load_w1(0, 0)
             list1 = load_list(offs, "list1")
             list2 = load_list(offs2, "list2")
-            list3 = load_list(offs3, "list3")
-            list4 = load_list(offs4, "list4")
             gains = keep.tile([P, R_PASSES, PACK], F32, name="gains")
             nc.sync.dma_start(gains[:], gain.rearrange("(b p t) -> p b t", p=P, t=PACK))
 
@@ -143,6 +141,8 @@ def tile_list_driveway_space_ledger_kernel(
         load_fit(0)
         load_fit(1)
         load_page(0)
+        list3 = load_list(offs3, "list3")
+        list4 = load_list(offs4, "list4")
         load_page(1)
         load_wgs(1)
         for a in range(K_PASSES):
@@ -180,7 +180,7 @@ def tile_list_driveway_space_ledger_kernel(
             if s >= VECTOR_SLICES:
                 for cols in halves:
                     nc.scalar.activation(spare[:, cols], h[:, cols], ACT.Tanh)
-                    nc.gpsimd.tensor_scalar(h[:, cols], spare[:, cols], gain_of(s), 0.0, ALU.mult, ALU.add)
+                    nc.scalar.activation(h[:, cols], spare[:, cols], ACT.Copy, scale=gain_of(s))
             elif s > 0:
                 nc.scalar.activation(h[:], h[:], ACT.Copy, scale=gain_of(s))
 

from contextlib import ExitStack

import concourse.mybir as mybir

K, T, S, H, T2, PAIRS, N = 1536, 4096, 1024, 1024, 2048, 512, 384
FLOPS = 2 * K * H * S + 2 * H * N * T2

F32 = mybir.dt.float32
BF16 = mybir.dt.bfloat16
I32 = mybir.dt.int32
U32 = mybir.dt.uint32
U16 = mybir.dt.uint16
U8 = mybir.dt.uint8
FP8X4 = mybir.dt.float8_e4m3fn_x4
FP4X4 = mybir.dt.float4_e2m1fn_x4
ALU = mybir.AluOpType
ACT = mybir.ActivationFunctionType

P = 128
PACK = 4
K_PASS = P * PACK
BANK = 512
BANKS = 8
LIST_ROWS = 16
QUAD = 32
SCALE_ROWS = 4
K_PASSES = K // K_PASS
R_PASSES = H // K_PASS
SLICES = R_PASSES * PACK
CHUNKS = T2 // BANK
M_TILES = N // P
GROUPS = CHUNKS * M_TILES
HALF_BANKS = BANKS // 2

QUADRANTS = (0, 2, 1, 3)
T_ORDER = (0, 2, 1, 3)
W1_BUFS, PAGE_BUFS, FIT_BUFS = K_PASSES, 4, 4
VECTOR_SLICES = 2


def slice_rows(s):
    return s // PACK, T_ORDER[s % PACK]


def tile_list_driveway_space_ledger_kernel(
    tc, tab_words, tab_scales, offs, w1, fit, gain, wgs, page0,
    offs2, offs3, offs4, w4_words, w4_scales, base, out,
):
    nc = tc.nc
    with ExitStack() as ctx:
        keep = ctx.enter_context(tc.tile_pool(name="keep", bufs=1))
        work = ctx.enter_context(tc.tile_pool(name="work", bufs=2))
        psum = ctx.enter_context(tc.psum_pool(name="psum", bufs=1))

        def load_list(source, name):
            listed = keep.tile(list(source.shape), U16, name=name)
            nc.sync.dma_start(listed[:], source)
            return listed

        banks = [psum.tile([P, BANK], F32, name="bank%d" % i) for i in range(BANKS)]
        woven = [keep.tile([P, BANK * PACK], BF16, name="woven%d" % c, align_bytes=64) for c in range(CHUNKS)]
        spare = keep.tile([P, S], F32, name="spare")
        weighed = [keep.tile([P, S], F32, name="weighed%d" % i, align_bytes=64) for i in range(2)]

        w1_raw, w1_codes, w1_scales = {}, {}, {}

        def load_w1(a, b):
            raw = work.tile([P, PACK, K_PASS], F32, name="w1_raw", bufs=W1_BUFS)
            rows = w1[K_PASS * a : K_PASS * (a + 1), K_PASS * b : K_PASS * (b + 1)]
            nc.sync.dma_start(raw[:], rows.rearrange("(p j) c -> p j c", j=PACK))
            w1_raw[a, b] = raw

        def quantise_w1(a, b, copy, grouped):
            copy(
                grouped.rearrange("p (t m j) -> p t m j", t=PACK, j=PACK),
                w1_raw[a, b][:].rearrange("p j (m t) -> p t m j", t=PACK),
            )
            codes = keep.tile([P, K_PASS], U32, name="w1_codes%d%d" % (a, b), align_bytes=64)
            scales = keep.tile([P, K_PASS], U8, name="w1_scales%d%d" % (a, b), align_bytes=64)
            nc.vector.quantize_mx(out=codes[:].bitcast(FP8X4), scales=scales[:], in_=grouped)
            w1_codes[a, b], w1_scales[a, b] = codes, scales

        fit_rows = fit.rearrange("(b p t) j -> b t p j", p=P, t=PACK)
        page_rows = page0.rearrange("(b p t) c -> b t p c", p=P, t=PACK)
        wgs_rows = wgs.rearrange("(m t) j -> t m j", t=PACK)
        fits, pages, dealt = {}, {}, {}

        def load_fit(s):
            fits[s] = work.tile([P, S], F32, name="fit_tile", bufs=FIT_BUFS)
            nc.sync.dma_start(fits[s][:], fit_rows[slice_rows(s)])

        def load_page(s):
            pages[s] = work.tile([P, T2], F32, name="page", bufs=PAGE_BUFS)
            nc.sync.dma_start(pages[s][:], page_rows[slice_rows(s)])

        def load_wgs(s):
            dealt[s] = keep.tile([P, S], F32, name="dealt%d" % s)
            for q in QUADRANTS:
                nc.sync.dma_start(dealt[s][QUAD * q : QUAD * (q + 1), :], wgs_rows[slice_rows(s)[1]])

        picked = [keep.tile([P, S], U32, name="picked%d" % a, align_bytes=64) for a in range(K_PASSES)]
        picked_scales = keep.tile([P, S], U8, name="picked_scales", align_bytes=64)

        with tc.tile_pool(name="table", bufs=1) as table:
            load_w1(0, 0)
            list1 = load_list(offs, "list1")
            list2 = load_list(offs2, "list2")
            gains = keep.tile([P, R_PASSES, PACK], F32, name="gains")
            nc.sync.dma_start(gains[:], gain.rearrange("(b p t) -> p b t", p=P, t=PACK))

            scale_rows = table.tile([P, T], U8, name="scale_rows")
            nc.vector.memset(scale_rows[:].bitcast(I32), 0)
            words = []
            for a in range(K_PASSES):
                if a > 0:
                    load_w1(a, 0)
                if a == 1:
                    for q in QUADRANTS:
                        nc.gpsimd.dma_start(
                            scale_rows[QUAD * q : QUAD * q + SCALE_ROWS * K_PASSES, :].bitcast(I32),
                            tab_scales[:, SCALE_ROWS * q : SCALE_ROWS * (q + 1), :].bitcast(I32),
                        )
                words.append(table.tile([P, T], U32, name="words%d" % a))
                nc.sync.dma_start(
                    words[a][:].bitcast(I32), tab_words[a].rearrange("p t i -> p (t i)").bitcast(I32)
                )
            for a in range(K_PASSES):
                quantise_w1(a, 0, nc.scalar.copy if a == 1 else nc.vector.tensor_copy, woven[a][:])
                if a == 1:
                    nc.vector.tensor_copy(picked_scales[:], scale_rows[:].indirect(list1[:]))
                width = BANK if a == K_PASSES - 1 else S
                for j0 in range(0, S, width):
                    nc.vector.tensor_copy(
                        picked[a][:, j0 : j0 + width],
                        words[a][:].indirect(list1[:, j0 // LIST_ROWS : (j0 + width) // LIST_ROWS]),
                    )

        late = ctx.enter_context(tc.tile_pool(name="late", bufs=1))

        load_wgs(0)
        load_fit(0)
        load_fit(1)
        load_page(0)
        list3 = load_list(offs3, "list3")
        list4 = load_list(offs4, "list4")
        load_page(1)
        load_wgs(1)
        for a in range(K_PASSES):
            load_w1(a, 1)
        load_page(2)
        load_wgs(2)
        load_fit(2)

        def gain_of(s):
            b, t = slice_rows(s)
            return gains[:, b, t : t + 1]

        def features(s):
            b, t = slice_rows(s)
            h = fits[s]
            halves = [slice(j0, j0 + BANK) for j0 in range(0, S, BANK)]
            for half, cols in enumerate(halves):
                acc = banks[len(halves) * (s % 2) + half]
                for a in range(K_PASSES):
                    nc.tensor.matmul_mx(
                        out=acc[:],
                        lhsT=w1_codes[a, b][:, P * t : P * (t + 1)].bitcast(FP8X4),
                        lhsT_scale=w1_scales[a, b][:, P * t : P * (t + 1)],
                        rhs=picked[a][:, cols].bitcast(FP8X4),
                        rhs_scale=picked_scales[SCALE_ROWS * a : P, cols],
                        start=(a == 0),
                        stop=(a == K_PASSES - 1),
                    )
                if s < VECTOR_SLICES:
                    nc.vector.tensor_tensor(h[:, cols], acc[:], h[:, cols], ALU.mult)
                    nc.scalar.activation(h[:, cols], h[:, cols], ACT.Tanh)
                else:
                    nc.scalar.copy(spare[:, cols], acc[:])
                    nc.gpsimd.tensor_tensor(h[:, cols], spare[:, cols], h[:, cols], ALU.mult)
            if s >= VECTOR_SLICES:
                for cols in halves:
                    nc.scalar.activation(spare[:, cols], h[:, cols], ACT.Tanh)
                    nc.scalar.activation(h[:, cols], spare[:, cols], ACT.Copy, scale=gain_of(s))
            elif s > 0:
                nc.scalar.activation(h[:], h[:], ACT.Copy, scale=gain_of(s))

        def weigh(s):
            nc.gpsimd.tensor_tensor(weighed[s % 2][:], fits[s][:], dealt[s % PACK][:], ALU.mult)

        def put_requests(s):
            nc.vector.tensor_copy(pages[s][:].indirect(list2[:]), weighed[s % 2][:])

        fetched, combined, sizes = {}, {}, {}

        def fetch_pairs(s):
            first = work.tile([P, PAIRS], F32, name="first", bufs=1)
            second = work.tile([P, PAIRS], F32, name="second", bufs=1)
            nc.vector.tensor_copy(first[:], pages[s][:].indirect(list3[:]))
            nc.vector.tensor_copy(second[:], pages[s][:].indirect(list4[:]))
            fetched[s] = (first, second)

        def combine(s):
            first, second = fetched[s]
            both = fits[s + 1] if s + 1 < SLICES else weighed[s % 2]
            nc.gpsimd.tensor_tensor(both[:, :PAIRS], first[:], second[:], ALU.add)
            nc.gpsimd.tensor_tensor(both[:, PAIRS:], first[:], second[:], ALU.subtract)
            combined[s] = both

        def put_sums(s):
            nc.vector.tensor_copy(pages[s][:].indirect(list4[:]), combined[s][:, :PAIRS])

        def take_sizes(s):
            sizes[s] = spare[:, PAIRS // 2 : PAIRS // 2 + PAIRS] if s + 2 < SLICES else combined[s][:, PAIRS:]
            nc.scalar.activation(sizes[s], combined[s][:, PAIRS:], ACT.Abs)

        def put_sizes(s):
            nc.vector.tensor_copy(pages[s][:].indirect(list3[:]), sizes[s])

        def round_page(s, c, copy):
            t = slice_rows(s)[1]
            copy(woven[c][:].rearrange("p (n t) -> p n t", t=PACK)[:, :, t], pages[s][:, BANK * c : BANK * (c + 1)])

        b_codes, b_scales = {}, {}

        def quantise_page(b, c):
            codes = keep.tile([P, BANK], U32, name="b_codes%d%d" % (b, c), align_bytes=64)
            scales = keep.tile([P, BANK], U8, name="b_scales%d%d" % (b, c), align_bytes=64)
            nc.vector.quantize_mx(out=codes[:].bitcast(FP8X4), scales=scales[:], in_=woven[c][:])
            b_codes[b, c], b_scales[b, c] = codes, scales

        w4_codes = keep.tile([P, R_PASSES, 2 * N], U8, name="w4_codes", align_bytes=64)
        w4_planes = keep.tile([P, R_PASSES, N], U8, name="w4_planes", align_bytes=64)
        bases = keep.tile([P, M_TILES], F32, name="bases")

        def load_w4():
            nc.vector.memset(w4_planes[:].bitcast(I32), 0)
            nc.sync.dma_start(w4_codes[:].bitcast(I32), w4_words.rearrange("a p c -> p a c").bitcast(I32))
            for q in range(P // QUAD):
                nc.sync.dma_start(
                    w4_planes[QUAD * q : QUAD * q + SCALE_ROWS, :, :].bitcast(I32),
                    w4_scales[:, SCALE_ROWS * q : SCALE_ROWS * (q + 1), :].rearrange("a r n -> r a n").bitcast(I32),
                )
            with nc.allow_non_contiguous_dma(reason="one bias value a partition"):
                nc.sync.dma_start(bases[:], base.rearrange("(m p) -> p m", p=P))

        def multiply_page(acc, g, b, start, stop):
            c, m = divmod(g, M_TILES)
            nc.tensor.matmul_mx(
                out=acc[:],
                lhsT=w4_codes[:, b, 2 * P * m : 2 * P * (m + 1)].bitcast(FP4X4),
                lhsT_scale=w4_planes[:, b, P * m : P * (m + 1)],
                rhs=b_codes[b, c][:].bitcast(FP8X4),
                rhs_scale=b_scales[b, c][:],
                start=start,
                stop=stop,
            )

        def add_base(result, acc, g):
            m = g % M_TILES
            nc.scalar.activation(result, acc[:], ACT.Identity, bias=bases[:, m : m + 1])

        nc.scalar.activation(weighed[0][:], dealt[0][:], ACT.Copy, scale=gain_of(0))
        features(0)
        features(1)
        nc.vector.tensor_tensor(pages[0][:].indirect(list2[:]), fits[0][:], weighed[0][:], ALU.mult)
        fetch_pairs(0)
        weigh(1)
        put_requests(1)
        combine(0)
        put_sums(0)
        fetch_pairs(1)
        for a in range(K_PASSES):
            if a + 1 < K_PASSES:
                grouped = late.tile([P, K_PASS * PACK], BF16, name="grouped%d" % a, align_bytes=64)
                quantise_w1(a, 1, nc.scalar.copy, grouped[:])
            else:
                quantise_w1(a, 1, nc.scalar.copy, weighed[0][:].bitcast(BF16))
        features(2)
        take_sizes(0)

        parked = {}
        for s in range(SLICES):
            if s + 3 < SLICES:
                load_page(s + 3)
                if s + 3 < PACK:
                    load_wgs(s + 3)
                load_fit(s + 3)
            if s == 1:
                load_w4()
            put_sizes(s)
            if s + 2 < SLICES:
                weigh(s + 2)
                put_requests(s + 2)
            if s + 1 < SLICES:
                combine(s + 1)
                put_sums(s + 1)
            if s + 2 < SLICES:
                fetch_pairs(s + 2)
            if s + 3 < SLICES:
                features(s + 3)
            if s + 1 < SLICES:
                take_sizes(s + 1)
                for c in range(CHUNKS):
                    round_page(s, c, nc.scalar.copy)
            if s == PACK - 1:
                for c in range(CHUNKS):
                    quantise_page(0, c)
            if s == PACK:
                for g in range(HALF_BANKS):
                    multiply_page(banks[HALF_BANKS + g], g, 0, True, False)
            if s == PACK + 1:
                for i in range(GROUPS - BANKS):
                    multiply_page(banks[i], BANKS + i, 0, True, True)
                    parked[BANKS + i] = (weighed[0], spare)[i // 2][:, BANK * (i % 2) : BANK * (i % 2 + 1)]
                    add_base(parked[BANKS + i], banks[i], BANKS + i)
                    multiply_page(banks[i], HALF_BANKS + i, 0, True, False)

        last = SLICES - 1
        round_page(last, CHUNKS - 1, nc.scalar.copy)
        round_page(last, 0, nc.vector.tensor_copy)
        for c in range(CHUNKS):
            if c + 1 < CHUNKS - 1:
                round_page(last, c + 1, nc.vector.tensor_copy)
            quantise_page(1, c)
        for g in range(GROUPS):
            c, m = divmod(g, M_TILES)
            result = late.tile([P, BANK], F32, name="result%d" % g)
            acc = banks[(g + HALF_BANKS) % BANKS]
            if g < BANKS:
                multiply_page(acc, g, 1, False, True)
                add_base(result[:], acc, g)
            else:
                multiply_page(acc, g, 1, True, True)
                nc.vector.tensor_tensor(result[:], acc[:], parked[g], ALU.add)
            nc.sync.dma_start(out[P * m : P * (m + 1), BANK * c : BANK * (c + 1)], result[:])
